import numpy as np
CORES = [35,38,43,46]
N = 4
T, SQ = 2048, 1024
def entries(a): return a.T.reshape(-1)
def pack(v, P): return np.ascontiguousarray(np.asarray(v, np.int32).reshape(-1, P).T)
def lists(rng, how):
    d = np.concatenate([[0], rng.integers(1 - SQ // 2, SQ // 2, N - 1), [int(rng.integers(1 - SQ // 2, 1))]])
    if how == "lag": d[1:] = -SQ
    if how == "lead": d[1:N] = SQ; d[N] = 0
    if how == "runs": m = int(rng.integers(1, N - 2)); d[m] = -abs(d[m]); d[m + 1] = d[m] + SQ; d[m + 2] = d[m]
    if how == "skew": t = int(rng.integers(2, N - 1)); d[1:] = rng.integers(SQ // 2 + 1, SQ - 1, N); d[t + 1:] *= -1; d[t] = d[t - 1] + d[t + 1]
    n = SQ + np.diff(d)
    F = np.zeros((N, T), np.int64)
    for r in range(N):
        o = rng.permutation(T)
        if how == "runs": o = (T // 16 * rng.permutation(16)[:, None] + np.arange(T // 16)).reshape(-1)
        if how == "skew": o = np.concatenate([[0, T - 1], 1 + rng.permutation(T - 2)])
        F[r, o[:n[r]]] = 1
    return {"fl": np.stack([pack(f, 16) for f in F])}
def setup_inputs(rng):
    return dict({"x": rng.standard_normal((N, 128, T), dtype=np.float32), "st": rng.standard_normal((N, 128, SQ), dtype=np.float32)}, **lists(rng, "uniform"))
def setup_inputs_lag(rng):
    d = setup_inputs(rng); d.update(lists(rng, "lag"))
    for k in ("x", "st"): d[k] = (d[k].astype(np.float32) * 1048576.0).astype(d[k].dtype)
    return d
def setup_inputs_lead(rng):
    d = setup_inputs(rng); d.update(lists(rng, "lead"))
    for k in ("x", "st"): d[k] = (d[k].astype(np.float32) * (1 / 1024.0)).astype(d[k].dtype)
    return d
def setup_inputs_runs(rng):
    d = setup_inputs(rng); d.update(lists(rng, "runs"))
    return d
def setup_inputs_skew(rng):
    d = setup_inputs(rng); d.update(lists(rng, "skew"))
    return d
def check_inputs(x):
    bad = []
    if x["fl"].min() < 0 or x["fl"].max() >= 2: bad.append("fl out of range")
    if int(x["fl"].sum()) > N * SQ: bad.append("more flags than the stream has columns")
    c = np.concatenate([[0], np.cumsum([int(a.sum()) for a in x["fl"]])])
    if any(c[r] < (r - 1) * SQ or c[r + 1] > (r + 2) * SQ for r in range(N)): bad.append("a rank's share of the stream reaches beyond its neighbours' parts")
    return bad
def reference(x, st, fl):
    S = np.concatenate(list(st), axis=1); X = np.concatenate(list(x), axis=1)
    F = np.concatenate([entries(f) for f in fl]) > 0; c = np.cumsum(F) - F
    Y = np.where(F[None, :], S[:, np.minimum(c, N * SQ - 1)], X)
    return {"y": np.stack([Y[:, T * r:T * r + T] for r in range(N)])}

from concourse.bass import DstId, RemoteDMATransfer
from concourse.mybir import dt, AluOpType, AxisListType, ActivationFunctionType

N, SQ, TC = 4, 1024, 2048
H = TC // 2
Q = 512
FW = 16

SCRATCH = {
    "win": ("sbuf", [128, 2 * H + 3 * SQ], "float32"),
    "yb": ("sbuf", [128, TC], "float32"),
    "fls": ("sbuf", [128, FW], "int32"),
    "flin": ("sbuf", [128, FW * N], "int32"),
    "flinb": ("sbuf", [128, FW * N], "bfloat16"),
    "f16": ("sbuf", [16, 128], "int32"),
    "fb": ("sbuf", [16, 128], "bfloat16"),
    "dm": ("sbuf", [16, 128], "float32"),
    "rep": ("sbuf", [16, 128], "bfloat16"),
    "bel": ("sbuf", [16, 128], "bfloat16"),
    "ones": ("sbuf", [128, 128], "bfloat16"),
    "pi": ("sbuf", [128, 4], "int32"),
    "pf": ("sbuf", [128, 4], "float32"),
    "xj": ("sbuf", [128, 128], "float32"),
    "zt": ("sbuf", [128, 128], "float32"),
    "ta": ("sbuf", [128, 128], "float32"),
    "tb": ("sbuf", [128, 128], "float32"),
    "base": ("sbuf", [128, 4], "float32"),
    "off": ("sbuf", [128, 128], "uint16"),
    "psum_s": ("psum", [128, 512], "float32"),
    "psum_b": ("psum", [128, 512], "float32"),
    "psum_r": ("psum", [128, 512], "float32"),
    "psum_c": ("psum", [128, 512], "float32"),
}
SEMAPHORES = ["l_fls", "l_f16", "l_st", "l_xa", "l_xb", "cst", "vec", "ten", "flg", "arrl", "arrr", "loc", "gate",
              "gv0", "gv1", "gs0", "gs1", "ysy", "ysc"]


def engines(mask):
    return [e for e in range(16) if (mask >> e) & 1]


def to_mask(es):
    m = 0
    for e in es:
        m |= 1 << e
    return m


def first_part(r):
    return max(r - 1, 0)


def section(r, part):
    return H + SQ * (part - first_part(r))


def off_chip(T, topo, a, b):
    return topo.chip(T.cores[a]) != topo.chip(T.cores[b])


def leave_mask(T, topo, a):
    for b in range(N):
        if off_chip(T, topo, a, b):
            return topo.mask(T.cores[a], T.cores[b])
    return 0


def stay_mask(T, topo, a):
    for b in range(N):
        if b != a and not off_chip(T, topo, a, b):
            return topo.mask(T.cores[a], T.cores[b]) & ~leave_mask(T, topo, a)
    return 0


def has_off_chip_neighbour(T, topo, a):
    return any(0 <= b < N and off_chip(T, topo, a, b) for b in (a - 1, a + 1))


def bulk_mask(T, topo, a, b):
    if off_chip(T, topo, a, b):
        return topo.mask(T.cores[a], T.cores[b])
    if has_off_chip_neighbour(T, topo, a):
        return stay_mask(T, topo, a)
    return to_mask(engines(topo.mask(T.cores[a], T.cores[b]))[::2])


def flag_mask(T, topo, a, b):
    if off_chip(T, topo, a, b):
        return leave_mask(T, topo, a)
    if any(off_chip(T, topo, a, q) for q in range(a + 1, N)):
        return to_mask(engines(stay_mask(T, topo, a))[::2])
    return leave_mask(T, topo, a)


def count(mask):
    return len(engines(mask))


def rank_program(g, core, T, topo):
    r = T.rank_of(core)
    if r is None:
        return
    A, S = AluOpType, T.sem
    parts = min(r + 1, N - 1) - first_part(r) + 1
    end = H + parts * SQ
    own = section(r, r)

    def dst(b):
        a = topo.addr(T.cores[b])
        return DstId(rid=a[0], pnc=a[1])

    if r < N - 1:
        g.sync.dma_start(T.fls[:], T.fl[:]).then_inc(S.l_fls, 16)
    g.sync.dma_start(T.win[:, own:own + SQ], T.st[:]).then_inc(S.l_st, 16)
    g.sync.dma_start(T.win[:, 0:H], T.x[:, 0:H]).then_inc(S.l_xa, 16)
    g.sync.wait_ge(S.gate, 1)
    g.sync.dma_start(T.win[:, end:end + H], T.x[:, H:TC]).then_inc(S.l_xb, 16)

    g.scalar.dma_start(T.f16[:], T.fl[:]).then_inc(S.l_f16, 16)

    g.iota(T.dm[:], [[0, 8], [1, 16]], 0, -1, allow_small_or_imprecise_dtypes=True).then_inc(S.cst, 1)
    g.iota(T.pi[:, 0:1], [[0, 1]], 0, 1).then_inc(S.cst, 1)
    g.iota(T.ta[:], [[parts * SQ, 2], [16, 64]], 0, 0, allow_small_or_imprecise_dtypes=True).then_inc(S.cst, 1)
    sent = 0
    if r < N - 1:
        g.wait_ge(S.l_fls, 16)
        groups = {}
        for b in range(r + 1, N):
            groups.setdefault(flag_mask(T, topo, r, b), []).append(b)
        tr = []
        land = T.flin[:, FW * r:FW * r + FW]
        for m, bs in groups.items():
            tr.append(RemoteDMATransfer(dst_ids=[dst(b) for b in bs], dma_engine_mask=m, remote_sem=S.flg,
                                        srcs=[T.fls[:]], dsts=[land for b in bs]))
            sent += count(m)
        g.remote_dma_fused(tr, local_sem=S.loc)
    g.wait_ge(S.l_st, 16)
    nb = [b for b in (r - 1, r + 1) if 0 <= b < N]
    nb.sort(key=lambda b: not off_chip(T, topo, r, b))
    for b in nb:
        m = bulk_mask(T, topo, r, b)
        c = section(b, r)
        rid, pid, _se = topo.addr(T.cores[b])
        g.remote_dma(T.win[:, c:c + SQ], T.win[:, own:own + SQ], S.arrl if r < b else S.arrr, S.loc, pid, rid, m)
        sent += count(m)
    g.sem_inc(S.gate, 1)
    g.wait_ge(S.loc, sent)

    n = [0]

    def v(call):
        call.then_inc(S.vec, 1)
        n[0] += 1
        g.vector.wait_ge(S.vec, n[0])

    v(g.vector.memset(T.ones[:], 1.0))
    v(g.vector.memset(T.zt[:], 0.0))
    v(g.vector.memset(T.zt[:, 64:65], float(-H)))
    g.vector.wait_ge(S.cst, 3)
    v(g.vector.tensor_scalar(T.rep[:], T.dm[:], 0.0, None, A.is_equal))
    v(g.vector.tensor_scalar(T.bel[:], T.dm[:], 0.0, -1.0, A.is_le, A.mult))
    v(g.vector.tensor_scalar(T.pi[:, 1:2], T.pi[:, 0:1], 15, None, A.bitwise_and))
    v(g.vector.tensor_copy(T.pf[:, 0:1], T.pi[:, 1:2]))
    v(g.vector.tensor_scalar(T.xj[:], T.ta[:], T.pf[:, 0:1], None, A.add))
    g.vector.wait_ge(S.l_f16, 16)
    v(g.vector.tensor_copy(T.fb[:], T.f16[:]))
    g.tensor.wait_ge(S.vec, n[0])
    g.tensor.matmul(T.psum_s[:, 0:128], T.ones[0:16, :], T.fb[:], True, True).then_inc(S.ten, 1)
    g.tensor.matmul(T.psum_b[:, 0:128], T.bel[:], T.fb[:], True, True).then_inc(S.ten, 1)
    g.tensor.matmul(T.psum_r[:, 0:128], T.rep[:], T.fb[:], True, True).then_inc(S.ten, 1)
    g.vector.wait_ge(S.ten, 3)
    v(g.vector.tensor_tensor_scan(T.ta[:], T.psum_s[:, 0:128], T.zt[:], float(H - SQ * first_part(r)), A.add, A.add))
    v(g.vector.tensor_tensor(T.ta[:], T.ta[:], T.psum_b[:, 0:128], A.add))
    v(g.vector.tensor_tensor(T.ta[:], T.ta[:], T.xj[:], A.subtract))
    v(g.vector.tensor_tensor(T.ta[:], T.ta[:], T.psum_r[:, 0:128], A.mult))
    v(g.vector.tensor_tensor(T.ta[:], T.ta[:], T.xj[:], A.add))
    if r > 0:
        w = FW * r
        g.vector.wait_ge(S.flg, sum(count(flag_mask(T, topo, a, r)) for a in range(r)))
        v(g.vector.tensor_copy(T.flinb[:, 0:w], T.flin[:, 0:w]))
        g.tensor.wait_ge(S.vec, n[0])
        g.tensor.matmul(T.psum_c[:, 0:w], T.ones[:], T.flinb[:, 0:w], True, True).then_inc(S.ten, 1)
        g.vector.wait_ge(S.ten, 4)
        v(g.vector.tensor_reduce(T.base[:, 0:1], T.psum_c[:, 0:w], AxisListType.X, A.add))
        v(g.vector.tensor_scalar(T.tb[:], T.psum_r[:, 0:128], T.base[:, 0:1], None, A.mult))
        v(g.vector.tensor_tensor(T.ta[:], T.ta[:], T.tb[:], A.add))
    v(g.vector.tensor_copy(T.off[:], T.ta[:]))

    def ready(q):
        q.wait_ge(S.l_st, 16)
        q.wait_ge(S.l_xa, 16)
        if r > 0:
            q.wait_ge(S.arrl, count(bulk_mask(T, topo, r - 1, r)))
        if r < N - 1:
            q.wait_ge(S.arrr, count(bulk_mask(T, topo, r + 1, r)))

    def win(half, k):
        cols = T.off[:, k * Q // 16:(k + 1) * Q // 16]
        return (T.win[:, 0:end] if half == 0 else T.win[:, H:end + H]).indirect(cols)

    def out(k):
        return T.yb[:, k * Q:(k + 1) * Q]

    ready(g.vector)
    g.vector.tensor_copy(out(0), win(0, 0)).then_inc(S.gv0, 1)
    g.vector.wait_ge(S.l_xb, 16)
    g.vector.tensor_copy(out(2), win(1, 2)).then_inc(S.gv1, 1)

    g.scalar.wait_ge(S.vec, n[0])
    ready(g.scalar)
    g.scalar.activation(out(1), win(0, 1), ActivationFunctionType.Copy).then_inc(S.gs0, 1)
    g.scalar.wait_ge(S.l_xb, 16)
    g.scalar.activation(out(3), win(1, 3), ActivationFunctionType.Copy).then_inc(S.gs1, 1)

    def store(q, k, made, done):
        q.wait_ge(made, 1)
        q.dma_start(T.y[:, k * Q:(k + 1) * Q], out(k)).then_inc(done, 16)

    store(g.sync, 0, S.gv0, S.ysy)
    store(g.sync, 1, S.gs0, S.ysy)
    store(g.sync, 2, S.gv1, S.ysy)
    store(g.scalar, 3, S.gs1, S.ysc)
    g.sync.wait_ge(S.ysy, 48)
    g.scalar.wait_ge(S.ysc, 16)
